import numpy as np
import ml_dtypes


def mxq(x, axis, fmt="e4m3"):
    dtype, down = {"e4m3": (ml_dtypes.float8_e4m3fn, 7), "e5m2": (ml_dtypes.float8_e5m2, 14)}[fmt]
    v = np.moveaxis(np.asarray(x, np.float32).astype(ml_dtypes.bfloat16).astype(np.float64), axis, -1)
    blocks = v.reshape(v.shape[:-1] + (-1, 32))
    amax = np.abs(blocks).max(-1, keepdims=True)
    byte = np.maximum(np.where(amax > 0, np.frexp(amax)[1] - 1 + 127, 0) - down, 1)
    scale = np.exp2(byte - 127.0)
    codes = (blocks / scale).astype(np.float32).astype(dtype).astype(np.float64)
    return np.moveaxis((codes * scale).reshape(v.shape), -1, axis)


WIDE = False


def mx_kscale(k):
    if not WIDE:
        return np.ones(k)
    levels = np.array([10, -10, 5, -5, 0])
    if k % 512:
        return np.exp2(np.random.permutation(np.resize(levels, k // 32))).repeat(32)
    a = np.empty((k // 512, 16))
    for p in range(k // 512):
        a[p, :8] = np.random.permutation(np.resize(levels, 8))
        for g in range(8):
            far = levels[np.abs(levels - a[p, g]) >= 10]
            a[p, g + 8] = far[np.random.randint(len(far))]
    return np.exp2(a.ravel()).repeat(32)


def f64(x):
    return np.asarray(x).astype(np.float64)


def striped(idx):
    return np.tile(np.asarray(idx).reshape(-1, 16).T, (8, 1)).astype(np.uint16)


def unstriped(offs):
    return offs[:16].T.reshape(-1).astype(np.int64)


R, K, T, I, G, F = 512, 512, 2048, 1024, 128, 512


def setup_inputs():
    n = np.random.standard_normal
    idx = np.random.permutation(T)[:I]
    fr = mx_kscale(R)
    fk = mx_kscale(K)
    return {
        "rad": (np.exp(-np.square(n((R, I)))) * fr[:, None]).astype(np.float32),
        "wr": (n((R, K)) * 1.5 / np.sqrt(R) / fr[:, None]).astype(np.float32),
        "atom": (n((K, T)) / fk[:, None]).astype(np.float32),
        "wo": (n((K, F)) * 0.4 / np.sqrt(K) * fk[:, None]).astype(np.float32),
        "offs": striped(idx),
    }


def reference(rad, wr, atom, wo, offs):
    idx = unstriped(offs)
    wrq = mxq(f64(wr), 0, "e4m3")
    radq = mxq(f64(rad), 0, "e4m3")
    z = wrq.T @ radq
    x = f64(atom)[:, idx] * z
    b = x.reshape(K, G, I // G).sum(axis=2)
    woq = mxq(f64(wo), 0, "e4m3")
    bq = mxq(b, 0, "e4m3")
    y = woq.T @ bq
    return y

@@ -1,0 +1,179 @@
+from contextlib import ExitStack
+
+import concourse.mybir as mybir
+from concourse.masks import make_identity
+
+R, K, T, I, G, F = 512, 512, 2048, 1024, 128, 512
+FLOPS = 2 * R * K * I + 2 * K * F * G
+
+F32 = mybir.dt.float32
+BF16 = mybir.dt.bfloat16
+U32 = mybir.dt.uint32
+U16 = mybir.dt.uint16
+U8 = mybir.dt.uint8
+FP8X4 = mybir.dt.float8_e4m3fn_x4
+MULT = mybir.AluOpType.mult
+ADD = mybir.AluOpType.add
+AXIS_X = mybir.AxisListType.X
+
+P = 128
+PACK = 4
+EDGES = I // G
+HALF = I // 2
+FH = F // 2
+PLANE_ORDER = (2, 0, 1, 3)
+WR_VECTOR_SHARE = 84
+RAD_VECTOR_SHARE = 84
+
+
+def tile_attend_filterconv_kernel(tc, rad, wr, atom, wo, offs, out):
+    nc = tc.nc
+    with ExitStack() as ctx:
+        keep = ctx.enter_context(tc.tile_pool(name="keep", bufs=1))
+        psum = ctx.enter_context(tc.psum_pool(name="psum", bufs=1))
+
+        offsets = keep.tile([P, I // 16], U16, name="offsets")
+        wr_raw = keep.tile([P, PACK, K], F32, name="wr_raw")
+        rad_raw = [keep.tile([P, PACK, HALF], F32, name="rad_raw%d" % h) for h in range(2)]
+        planes = {t: keep.tile([P, T], F32, name="atom%d" % t) for t in PLANE_ORDER}
+        wo_raw = [keep.tile([P, PACK, FH], F32, name="wo_raw%d" % h) for h in range(2)]
+
+        rad_rows = rad.rearrange("(p j) i -> p j i", j=PACK)
+        atom_rows = atom.rearrange("(p t) c -> p t c", t=PACK)
+        wo_rows = wo.rearrange("(p j) f -> p j f", j=PACK)
+        nc.sync.dma_start(out=wr_raw[:], in_=wr.rearrange("(p j) k -> p j k", j=PACK))
+        nc.sync.dma_start(offsets[:], offs)
+        for h in range(2):
+            nc.sync.dma_start(out=rad_raw[h][:], in_=rad_rows[:, :, h * HALF : (h + 1) * HALF])
+        for t in PLANE_ORDER:
+            nc.sync.dma_start(out=planes[t][:], in_=atom_rows[:, t, :])
+        for h in range(2):
+            nc.sync.dma_start(out=wo_raw[h][:], in_=wo_rows[:, :, h * FH : (h + 1) * FH])
+
+        ident = keep.tile([P, P], F32, name="ident")
+        make_identity(nc, ident[:])
+
+        def quantize(src, width, name):
+            codes = keep.tile([P, width], U32, name=name + "_codes", align_bytes=64)
+            scales = keep.tile([P, width], U8, name=name + "_scales", align_bytes=64)
+            nc.vector.quantize_mx(out=codes[:].bitcast(FP8X4), scales=scales[:], in_=src)
+            return codes, scales
+
+        def interleave(raw, grouped, vector_share):
+            src = raw[:].rearrange("p j (c i) -> p c j i", i=4)
+            dst = grouped[:].rearrange("p (c i j) -> p c j i", i=4, j=PACK)
+            groups = src.shape[1]
+            if vector_share > 0:
+                nc.vector.tensor_copy(out=dst[:, :vector_share], in_=src[:, :vector_share])
+            if vector_share < groups:
+                nc.scalar.copy(out=dst[:, vector_share:], in_=src[:, vector_share:])
+
+        wr_bf = keep.tile([P, K * PACK], BF16, name="wr_bf", align_bytes=64)
+        src = wr_raw[:].rearrange("p j (m t) -> p m j t", t=PACK)
+        dst = wr_bf[:].rearrange("p (t m j) -> p m j t", t=PACK, j=PACK)
+        nc.vector.tensor_copy(out=dst[:, :WR_VECTOR_SHARE], in_=src[:, :WR_VECTOR_SHARE])
+        nc.scalar.copy(out=dst[:, WR_VECTOR_SHARE:], in_=src[:, WR_VECTOR_SHARE:])
+        wr_codes, wr_scales = quantize(wr_bf[:], K, "wr")
+
+        z = {t: keep.tile([P, I], F32, name="z%d" % t) for t in PLANE_ORDER}
+        rad_q = []
+
+        def filter_tile(t, h, tag, bufs):
+            bank = psum.tile([P, HALF], F32, name="zbank", tag=tag, bufs=bufs)
+            codes, scales = rad_q[h]
+            nc.tensor.matmul_mx(
+                out=bank[:],
+                lhsT=wr_codes[:, t * P : (t + 1) * P].bitcast(FP8X4),
+                lhsT_scale=wr_scales[:, t * P : (t + 1) * P],
+                rhs=codes[:].bitcast(FP8X4),
+                rhs_scale=scales[:],
+                start=True,
+                stop=True,
+            )
+            nc.scalar.copy(out=z[t][:, h * HALF : (h + 1) * HALF], in_=bank[:])
+
+        last = PLANE_ORDER[-1]
+        for h in range(2):
+            rad_bf = keep.tile([P, HALF * PACK], BF16, name="rad_bf%d" % h, align_bytes=64)
+            interleave(rad_raw[h], rad_bf, RAD_VECTOR_SHARE if h == 0 else HALF // 4)
+            rad_q.append(quantize(rad_bf[:], HALF, "rad%d" % h))
+            for t in PLANE_ORDER:
+                if (t, h) != (last, 1):
+                    filter_tile(t, h, "z", 4)
+
+        b_bf = keep.tile([P, G, PACK], BF16, name="b_bf", align_bytes=64)
+        x = {t: keep.tile([P, I], F32, name="x%d" % t) for t in PLANE_ORDER}
+
+        def products(t):
+            for h in range(2):
+                cols = slice(h * HALF, (h + 1) * HALF)
+                listed = planes[t][:].indirect(offsets[:, h * HALF // 16 : (h + 1) * HALF // 16])
+                nc.vector.tensor_tensor(x[t][:, cols], listed, z[t][:, cols], MULT)
+
+        def turn(t):
+            turned = psum.tile([G, P], F32, name="turned", tag="turned", bufs=2)
+            for e in range(EDGES):
+                nc.tensor.matmul(
+                    turned[:], x[t][:, e::EDGES], ident[:], start=(e == 0), stop=(e == EDGES - 1), is_transpose=True
+                )
+            return turned
+
+        def turn_back(t, staged, tag):
+            back = psum.tile([P, G], F32, name="back", tag=tag, bufs=1)
+            nc.tensor.transpose(back[:], staged, ident[:])
+            nc.scalar.copy(out=b_bf[:, :, t], in_=back[:])
+
+        for n, t in enumerate(PLANE_ORDER[:2]):
+            products(t)
+            turned = turn(t)
+            staged = keep.tile([G, P], F32, name="staged%d" % t)
+            nc.scalar.copy(out=staged[:], in_=turned[:])
+            turn_back(t, staged[:], "late" if n == 0 else "back")
+            if n == 0:
+                filter_tile(last, 1, "late", 1)
+        third = PLANE_ORDER[2]
+        products(third)
+        turned = turn(third)
+
+        wo_bf = [keep.tile([P, FH * PACK], BF16, name="wo_bf%d" % h, align_bytes=64) for h in range(2)]
+        products(last)
+        interleave(wo_raw[0], wo_bf[0], 0)
+        src = wo_raw[1][:].rearrange("p j (c i) -> p c j i", i=4)
+        dst = wo_bf[1][:].rearrange("p (c i j) -> p c j i", i=4, j=PACK)
+        nc.scalar.copy(out=dst[:, : P // 4], in_=src[:, : P // 4])
+        staged = wo_raw[1][:, 0, :P]
+        nc.scalar.copy(out=staged, in_=turned[:])
+        nc.scalar.copy(out=dst[:, P // 4 :], in_=src[:, P // 4 :])
+        turn_back(third, staged, "back")
+        with nc.allow_low_precision(reason="float32 sum, rounded once for the quantiser"):
+            for h in range(2):
+                nc.vector.tensor_reduce(
+                    out=b_bf[:, h * G // 2 : (h + 1) * G // 2, last],
+                    in_=x[last][:, h * HALF : (h + 1) * HALF].rearrange("p (g e) -> p g e", e=EDGES),
+                    axis=AXIS_X,
+                    op=ADD,
+                )
+        wo_q0 = quantize(wo_bf[0][:], FH, "wo0")
+        wo_q1 = quantize(wo_bf[1][:], FH, "wo1")
+        b_codes, b_scales = quantize(b_bf[:].rearrange("p g t -> p (g t)"), G, "b")
+
+        out_rows = out.rearrange("(j p) g -> p j g", p=P)
+        for h, (codes, scales) in enumerate((wo_q0, wo_q1)):
+            bank = psum.tile([P, 2, G], F32, name="ybank", tag="z", bufs=4)
+            for j in range(2):
+                nc.tensor.matmul_mx(
+                    out=bank[:, j, :],
+                    lhsT=codes[:, j * P : (j + 1) * P].bitcast(FP8X4),
+                    lhsT_scale=scales[:, j * P : (j + 1) * P],
+                    rhs=b_codes[:].bitcast(FP8X4),
+                    rhs_scale=b_scales[:],
+                    start=True,
+                    stop=True,
+                )
+            y = keep.tile([P, 2, G], F32, name="y%d" % h)
+            if h == 0:
+                nc.scalar.copy(out=y[:], in_=bank[:])
+                nc.scalar.dma_start(out=out_rows[:, 0:2, :], in_=y[:])
+            else:
+                nc.vector.tensor_copy(out=y[:], in_=bank[:])
+                nc.sync.dma_start(out=out_rows[:, 2:4, :], in_=y[:])

@@ -69,8 +69,8 @@ def tile_attend_filterconv_kernel(tc, rad, wr, atom, wo, offs, out):
                 nc.scalar.copy(out=dst[:, vector_share:], in_=src[:, vector_share:])
 
         wr_bf = keep.tile([P, K * PACK], BF16, name="wr_bf", align_bytes=64)
-        src = wr_raw[:].rearrange("p j (m t) -> p m j t", t=PACK)
-        dst = wr_bf[:].rearrange("p (t m j) -> p m j t", t=PACK, j=PACK)
+        src = wr_raw[:].rearrange("p j (m t) -> p m t j", t=PACK)
+        dst = wr_bf[:].rearrange("p (t m j) -> p m t j", t=PACK, j=PACK)
         nc.vector.tensor_copy(out=dst[:, :WR_VECTOR_SHARE], in_=src[:, :WR_VECTOR_SHARE])
         nc.scalar.copy(out=dst[:, WR_VECTOR_SHARE:], in_=src[:, WR_VECTOR_SHARE:])
         wr_codes, wr_scales = quantize(wr_bf[:], K, "wr")
@@ -90,7 +90,7 @@ def tile_attend_filterconv_kernel(tc, rad, wr, atom, wo, offs, out):
                 start=True,
                 stop=True,
             )
-            nc.scalar.copy(out=z[t][:, h * HALF : (h + 1) * HALF], in_=bank[:])
+            return bank
 
         last = PLANE_ORDER[-1]
         for h in range(2):
@@ -98,8 +98,10 @@ def tile_attend_filterconv_kernel(tc, rad, wr, atom, wo, offs, out):
             interleave(rad_raw[h], rad_bf, RAD_VECTOR_SHARE if h == 0 else HALF // 4)
             rad_q.append(quantize(rad_bf[:], HALF, "rad%d" % h))
             for t in PLANE_ORDER:
+                bank = filter_tile(t, h, "z", 4)
                 if (t, h) != (last, 1):
-                    filter_tile(t, h, "z", 4)
+                    nc.scalar.copy(out=z[t][:, h * HALF : (h + 1) * HALF], in_=bank[:])
+        held = bank
 
         b_bf = keep.tile([P, G, PACK], BF16, name="b_bf", align_bytes=64)
         x = {t: keep.tile([P, I], F32, name="x%d" % t) for t in PLANE_ORDER}
@@ -111,27 +113,27 @@ def tile_attend_filterconv_kernel(tc, rad, wr, atom, wo, offs, out):
                 nc.vector.tensor_tensor(x[t][:, cols], listed, z[t][:, cols], MULT)
 
         def turn(t):
-            turned = psum.tile([G, P], F32, name="turned", tag="turned", bufs=2)
+            turned = psum.tile([G, P], F32, name="turned", tag="sums%d" % t, bufs=1)
             for e in range(EDGES):
                 nc.tensor.matmul(
                     turned[:], x[t][:, e::EDGES], ident[:], start=(e == 0), stop=(e == EDGES - 1), is_transpose=True
                 )
             return turned
 
-        def turn_back(t, staged, tag):
-            back = psum.tile([P, G], F32, name="back", tag=tag, bufs=1)
-            nc.tensor.transpose(back[:], staged, ident[:])
-            nc.scalar.copy(out=b_bf[:, :, t], in_=back[:])
+        first, second, third = PLANE_ORDER[:3]
+        products(first)
+        turned = turn(first)
+        staged = z[last][:, HALF : HALF + P]
+        nc.scalar.copy(out=staged, in_=turned[:])
+        back = psum.tile([P, G], F32, name="back", tag="sums%d" % first, bufs=1)
+        nc.tensor.transpose(back[:], staged, ident[:])
+        nc.scalar.copy(out=b_bf[:, :, first], in_=back[:])
+        nc.scalar.copy(out=z[last][:, HALF:], in_=held[:])
 
-        for n, t in enumerate(PLANE_ORDER[:2]):
-            products(t)
-            turned = turn(t)
-            staged = keep.tile([G, P], F32, name="staged%d" % t)
-            nc.scalar.copy(out=staged[:], in_=turned[:])
-            turn_back(t, staged[:], "late" if n == 0 else "back")
-            if n == 0:
-                filter_tile(last, 1, "late", 1)
-        third = PLANE_ORDER[2]
+        products(second)
+        turned = turn(second)
+        staged_second = keep.tile([G, P], F32, name="staged_second")
+        nc.scalar.copy(out=staged_second[:], in_=turned[:])
         products(third)
         turned = turn(third)
 
@@ -144,7 +146,10 @@ def tile_attend_filterconv_kernel(tc, rad, wr, atom, wo, offs, out):
         staged = wo_raw[1][:, 0, :P]
         nc.scalar.copy(out=staged, in_=turned[:])
         nc.scalar.copy(out=dst[:, P // 4 :], in_=src[:, P // 4 :])
-        turn_back(third, staged, "back")
+        back = psum.tile([P, 2, G], F32, name="back", tag="sums%d" % third, bufs=1)
+        nc.tensor.transpose(back[:, 0, :], staged_second[:], ident[:])
+        nc.tensor.transpose(back[:, 1, :], staged, ident[:])
+        nc.scalar.copy(out=b_bf[:, :, 0:2], in_=back[:].rearrange("p t g -> p g t"))
         with nc.allow_low_precision(reason="float32 sum, rounded once for the quantiser"):
             for h in range(2):
                 nc.vector.tensor_reduce(

@@ -140,12 +140,19 @@ def tile_attend_filterconv_kernel(tc, rad, wr, atom, wo, offs, out):
         wo_bf = [keep.tile([P, FH * PACK], BF16, name="wo_bf%d" % h, align_bytes=64) for h in range(2)]
         products(last)
         interleave(wo_raw[0], wo_bf[0], 0)
+        staged = wo_raw[0][:, 0, :P]
+        nc.scalar.copy(out=staged, in_=turned[:])
         src = wo_raw[1][:].rearrange("p j (c i) -> p c j i", i=4)
         dst = wo_bf[1][:].rearrange("p (c i j) -> p c j i", i=4, j=PACK)
         nc.scalar.copy(out=dst[:, : P // 4], in_=src[:, : P // 4])
-        staged = wo_raw[1][:, 0, :P]
-        nc.scalar.copy(out=staged, in_=turned[:])
-        nc.scalar.copy(out=dst[:, P // 4 :], in_=src[:, P // 4 :])
+        nc.gpsimd.tensor_scalar(
+            wo_bf[1][:].rearrange("p (f j) -> p f j", j=PACK)[:, P:],
+            wo_raw[1][:].rearrange("p j f -> p f j")[:, P:],
+            1.0,
+            0.0,
+            MULT,
+            ADD,
+        )
         back = psum.tile([P, 2, G], F32, name="back", tag="sums%d" % third, bufs=1)
         nc.tensor.transpose(back[:, 0, :], staged_second[:], ident[:])
         nc.tensor.transpose(back[:, 1, :], staged, ident[:])

@@ -23,7 +23,7 @@ HALF = I // 2
 FH = F // 2
 PLANE_ORDER = (2, 0, 1, 3)
 WR_VECTOR_SHARE = 84
-RAD_VECTOR_SHARE = 84
+RAD_VECTOR_SHARE = 80
 
 
 def tile_attend_filterconv_kernel(tc, rad, wr, atom, wo, offs, out):
@@ -34,7 +34,7 @@ def tile_attend_filterconv_kernel(tc, rad, wr, atom, wo, offs, out):
 
         offsets = keep.tile([P, I // 16], U16, name="offsets")
         wr_raw = keep.tile([P, PACK, K], F32, name="wr_raw")
-        rad_raw = [keep.tile([P, PACK, HALF], F32, name="rad_raw%d" % h) for h in range(2)]
+        rad_raw = [keep.tile([P, PACK, HALF], F32, name="rad_raw%d" % h, tag="rad_raw%d" % h) for h in range(2)]
         planes = {t: keep.tile([P, T], F32, name="atom%d" % t) for t in PLANE_ORDER}
         wo_raw = [keep.tile([P, PACK, FH], F32, name="wo_raw%d" % h) for h in range(2)]
 
@@ -75,11 +75,10 @@ def tile_attend_filterconv_kernel(tc, rad, wr, atom, wo, offs, out):
         nc.scalar.copy(out=dst[:, WR_VECTOR_SHARE:], in_=src[:, WR_VECTOR_SHARE:])
         wr_codes, wr_scales = quantize(wr_bf[:], K, "wr")
 
-        z = {t: keep.tile([P, I], F32, name="z%d" % t) for t in PLANE_ORDER}
         rad_q = []
 
-        def filter_tile(t, h, tag, bufs):
-            bank = psum.tile([P, HALF], F32, name="zbank", tag=tag, bufs=bufs)
+        def filter_tile(t, h):
+            bank = psum.tile([P, HALF], F32, name="zbank", tag="bank%d" % (2 * t + h))
             codes, scales = rad_q[h]
             nc.tensor.matmul_mx(
                 out=bank[:],
@@ -95,25 +94,28 @@ def tile_attend_filterconv_kernel(tc, rad, wr, atom, wo, offs, out):
         last = PLANE_ORDER[-1]
         for h in range(2):
             rad_bf = keep.tile([P, HALF * PACK], BF16, name="rad_bf%d" % h, align_bytes=64)
-            interleave(rad_raw[h], rad_bf, RAD_VECTOR_SHARE if h == 0 else HALF // 4)
+            interleave(rad_raw[h], rad_bf, RAD_VECTOR_SHARE)
             rad_q.append(quantize(rad_bf[:], HALF, "rad%d" % h))
-            for t in PLANE_ORDER:
-                bank = filter_tile(t, h, "z", 4)
+        z = keep.tile([P, PACK, I], F32, name="z", tag="rad_raw1")
+        for t in PLANE_ORDER:
+            for h in range(2):
+                bank = filter_tile(t, h)
                 if (t, h) != (last, 1):
-                    nc.scalar.copy(out=z[t][:, h * HALF : (h + 1) * HALF], in_=bank[:])
+                    nc.scalar.copy(out=z[:, t, h * HALF : (h + 1) * HALF], in_=bank[:])
         held = bank
 
         b_bf = keep.tile([P, G, PACK], BF16, name="b_bf", align_bytes=64)
         x = {t: keep.tile([P, I], F32, name="x%d" % t) for t in PLANE_ORDER}
 
-        def products(t):
-            for h in range(2):
-                cols = slice(h * HALF, (h + 1) * HALF)
-                listed = planes[t][:].indirect(offsets[:, h * HALF // 16 : (h + 1) * HALF // 16])
-                nc.vector.tensor_tensor(x[t][:, cols], listed, z[t][:, cols], MULT)
+        def products(t, pieces):
+            width = I // pieces
+            for h in range(pieces):
+                cols = slice(h * width, (h + 1) * width)
+                listed = planes[t][:].indirect(offsets[:, h * width // 16 : (h + 1) * width // 16])
+                nc.vector.tensor_tensor(x[t][:, cols], listed, z[:, t, cols], MULT)
 
         def turn(t):
-            turned = psum.tile([G, P], F32, name="turned", tag="sums%d" % t, bufs=1)
+            turned = psum.tile([G, P], F32, name="turned", tag="bank%d" % (2 * t))
             for e in range(EDGES):
                 nc.tensor.matmul(
                     turned[:], x[t][:, e::EDGES], ident[:], start=(e == 0), stop=(e == EDGES - 1), is_transpose=True
@@ -121,24 +123,24 @@ def tile_attend_filterconv_kernel(tc, rad, wr, atom, wo, offs, out):
             return turned
 
         first, second, third = PLANE_ORDER[:3]
-        products(first)
+        products(first, 2)
         turned = turn(first)
-        staged = z[last][:, HALF : HALF + P]
+        staged = z[:, last, HALF : HALF + P]
         nc.scalar.copy(out=staged, in_=turned[:])
-        back = psum.tile([P, G], F32, name="back", tag="sums%d" % first, bufs=1)
+        back = psum.tile([P, G], F32, name="back", tag="bank%d" % (2 * first))
         nc.tensor.transpose(back[:], staged, ident[:])
         nc.scalar.copy(out=b_bf[:, :, first], in_=back[:])
-        nc.scalar.copy(out=z[last][:, HALF:], in_=held[:])
+        nc.scalar.copy(out=z[:, last, HALF:], in_=held[:])
 
-        products(second)
+        products(second, 1)
         turned = turn(second)
         staged_second = keep.tile([G, P], F32, name="staged_second")
         nc.scalar.copy(out=staged_second[:], in_=turned[:])
-        products(third)
+        products(third, 1)
         turned = turn(third)
 
         wo_bf = [keep.tile([P, FH * PACK], BF16, name="wo_bf%d" % h, align_bytes=64) for h in range(2)]
-        products(last)
+        products(last, 2)
         interleave(wo_raw[0], wo_bf[0], 0)
         staged = wo_raw[0][:, 0, :P]
         nc.scalar.copy(out=staged, in_=turned[:])
@@ -153,7 +155,7 @@ def tile_attend_filterconv_kernel(tc, rad, wr, atom, wo, offs, out):
             MULT,
             ADD,
         )
-        back = psum.tile([P, 2, G], F32, name="back", tag="sums%d" % third, bufs=1)
+        back = psum.tile([P, 2, G], F32, name="back", tag="bank%d" % (2 * third))
         nc.tensor.transpose(back[:, 0, :], staged_second[:], ident[:])
         nc.tensor.transpose(back[:, 1, :], staged, ident[:])
         nc.scalar.copy(out=b_bf[:, :, 0:2], in_=back[:].rearrange("p t g -> p g t"))
@@ -170,22 +172,29 @@ def tile_attend_filterconv_kernel(tc, rad, wr, atom, wo, offs, out):
         b_codes, b_scales = quantize(b_bf[:].rearrange("p g t -> p (g t)"), G, "b")
 
         out_rows = out.rearrange("(j p) g -> p j g", p=P)
-        for h, (codes, scales) in enumerate((wo_q0, wo_q1)):
-            bank = psum.tile([P, 2, G], F32, name="ybank", tag="z", bufs=4)
-            for j in range(2):
-                nc.tensor.matmul_mx(
-                    out=bank[:, j, :],
-                    lhsT=codes[:, j * P : (j + 1) * P].bitcast(FP8X4),
-                    lhsT_scale=scales[:, j * P : (j + 1) * P],
-                    rhs=b_codes[:].bitcast(FP8X4),
-                    rhs_scale=b_scales[:],
-                    start=True,
-                    stop=True,
-                )
-            y = keep.tile([P, 2, G], F32, name="y%d" % h)
-            if h == 0:
-                nc.scalar.copy(out=y[:], in_=bank[:])
-                nc.scalar.dma_start(out=out_rows[:, 0:2, :], in_=y[:])
+        def output_tile(acc, wo_q, j):
+            codes, scales = wo_q
+            nc.tensor.matmul_mx(
+                out=acc,
+                lhsT=codes[:, j * P : (j + 1) * P].bitcast(FP8X4),
+                lhsT_scale=scales[:, j * P : (j + 1) * P],
+                rhs=b_codes[:].bitcast(FP8X4),
+                rhs_scale=b_scales[:],
+                start=True,
+                stop=True,
+            )
+
+        y = [keep.tile([P, 2, G], F32, name="y%d" % h) for h in range(2)]
+        bank = psum.tile([P, 2, G], F32, name="ybank", tag="bank1")
+        for j in range(2):
+            output_tile(bank[:, j, :], wo_q0, j)
+        nc.scalar.copy(out=y[0][:], in_=bank[:])
+        nc.sync.dma_start(out=out_rows[:, 0:2, :], in_=y[0][:])
+        for j in range(2):
+            bank = psum.tile([P, G], F32, name="ybank", tag="bank%d" % (3 + 2 * j))
+            output_tile(bank[:], wo_q1, j)
+            if j == 0:
+                nc.vector.tensor_copy(out=y[1][:, j, :], in_=bank[:])
             else:
-                nc.vector.tensor_copy(out=y[:], in_=bank[:])
-                nc.sync.dma_start(out=out_rows[:, 2:4, :], in_=y[:])
+                nc.scalar.copy(out=y[1][:, j, :], in_=bank[:])
+        nc.sync.dma_start(out=out_rows[:, 2:4, :], in_=y[1][:])

from contextlib import ExitStack

import concourse.mybir as mybir
from concourse.masks import make_identity

R, K, T, I, G, F = 512, 512, 2048, 1024, 128, 512
FLOPS = 2 * R * K * I + 2 * K * F * G

F32 = mybir.dt.float32
BF16 = mybir.dt.bfloat16
U32 = mybir.dt.uint32
U16 = mybir.dt.uint16
U8 = mybir.dt.uint8
FP8X4 = mybir.dt.float8_e4m3fn_x4
MULT = mybir.AluOpType.mult
ADD = mybir.AluOpType.add
AXIS_X = mybir.AxisListType.X

P = 128
PACK = 4
EDGES = I // G
HALF = I // 2
FH = F // 2
PLANE_ORDER = (2, 0, 1, 3)
WR_VECTOR_SHARE = 84
RAD_VECTOR_SHARE = 80


def tile_attend_filterconv_kernel(tc, rad, wr, atom, wo, offs, out):
    nc = tc.nc
    with ExitStack() as ctx:
        keep = ctx.enter_context(tc.tile_pool(name="keep", bufs=1))
        psum = ctx.enter_context(tc.psum_pool(name="psum", bufs=1))

        offsets = keep.tile([P, I // 16], U16, name="offsets")
        wr_raw = keep.tile([P, PACK, K], F32, name="wr_raw")
        rad_raw = [keep.tile([P, PACK, HALF], F32, name="rad_raw%d" % h, tag="rad_raw%d" % h) for h in range(2)]
        planes = {t: keep.tile([P, T], F32, name="atom%d" % t) for t in PLANE_ORDER}
        wo_raw = [keep.tile([P, PACK, FH], F32, name="wo_raw%d" % h) for h in range(2)]

        rad_rows = rad.rearrange("(p j) i -> p j i", j=PACK)
        atom_rows = atom.rearrange("(p t) c -> p t c", t=PACK)
        wo_rows = wo.rearrange("(p j) f -> p j f", j=PACK)
        nc.sync.dma_start(out=wr_raw[:], in_=wr.rearrange("(p j) k -> p j k", j=PACK))
        nc.sync.dma_start(offsets[:], offs)
        for h in range(2):
            nc.sync.dma_start(out=rad_raw[h][:], in_=rad_rows[:, :, h * HALF : (h + 1) * HALF])
        for t in PLANE_ORDER:
            nc.sync.dma_start(out=planes[t][:], in_=atom_rows[:, t, :])
        for h in range(2):
            nc.sync.dma_start(out=wo_raw[h][:], in_=wo_rows[:, :, h * FH : (h + 1) * FH])

        ident = keep.tile([P, P], F32, name="ident")
        make_identity(nc, ident[:])

        def quantize(src, width, name):
            codes = keep.tile([P, width], U32, name=name + "_codes", align_bytes=64)
            scales = keep.tile([P, width], U8, name=name + "_scales", align_bytes=64)
            nc.vector.quantize_mx(out=codes[:].bitcast(FP8X4), scales=scales[:], in_=src)
            return codes, scales

        def interleave(raw, grouped, vector_share):
            src = raw[:].rearrange("p j (c i) -> p c j i", i=4)
            dst = grouped[:].rearrange("p (c i j) -> p c j i", i=4, j=PACK)
            groups = src.shape[1]
            if vector_share > 0:
                nc.vector.tensor_copy(out=dst[:, :vector_share], in_=src[:, :vector_share])
            if vector_share < groups:
                nc.scalar.copy(out=dst[:, vector_share:], in_=src[:, vector_share:])

        wr_bf = keep.tile([P, K * PACK], BF16, name="wr_bf", align_bytes=64)
        src = wr_raw[:].rearrange("p j (m t) -> p m t j", t=PACK)
        dst = wr_bf[:].rearrange("p (t m j) -> p m t j", t=PACK, j=PACK)
        nc.vector.tensor_copy(out=dst[:, :WR_VECTOR_SHARE], in_=src[:, :WR_VECTOR_SHARE])
        nc.scalar.copy(out=dst[:, WR_VECTOR_SHARE:], in_=src[:, WR_VECTOR_SHARE:])
        wr_codes, wr_scales = quantize(wr_bf[:], K, "wr")

        rad_q = []

        def filter_tile(t, h):
            bank = psum.tile([P, HALF], F32, name="zbank", tag="bank%d" % (2 * t + h))
            codes, scales = rad_q[h]
            nc.tensor.matmul_mx(
                out=bank[:],
                lhsT=wr_codes[:, t * P : (t + 1) * P].bitcast(FP8X4),
                lhsT_scale=wr_scales[:, t * P : (t + 1) * P],
                rhs=codes[:].bitcast(FP8X4),
                rhs_scale=scales[:],
                start=True,
                stop=True,
            )
            return bank

        last = PLANE_ORDER[-1]
        for h in range(2):
            rad_bf = keep.tile([P, HALF * PACK], BF16, name="rad_bf%d" % h, align_bytes=64)
            interleave(rad_raw[h], rad_bf, RAD_VECTOR_SHARE)
            rad_q.append(quantize(rad_bf[:], HALF, "rad%d" % h))
        z = keep.tile([P, PACK, I], F32, name="z", tag="rad_raw1")
        for t in PLANE_ORDER:
            for h in range(2):
                bank = filter_tile(t, h)
                if (t, h) != (last, 1):
                    nc.scalar.copy(out=z[:, t, h * HALF : (h + 1) * HALF], in_=bank[:])
        held = bank

        b_bf = keep.tile([P, G, PACK], BF16, name="b_bf", align_bytes=64)
        x = {t: keep.tile([P, I], F32, name="x%d" % t) for t in PLANE_ORDER}

        def products(t, pieces):
            width = I // pieces
            for h in range(pieces):
                cols = slice(h * width, (h + 1) * width)
                listed = planes[t][:].indirect(offsets[:, h * width // 16 : (h + 1) * width // 16])
                nc.vector.tensor_tensor(x[t][:, cols], listed, z[:, t, cols], MULT)

        def turn(t):
            turned = psum.tile([G, P], F32, name="turned", tag="bank%d" % (2 * t))
            for e in range(EDGES):
                nc.tensor.matmul(
                    turned[:], x[t][:, e::EDGES], ident[:], start=(e == 0), stop=(e == EDGES - 1), is_transpose=True
                )
            return turned

        first, second, third = PLANE_ORDER[:3]
        products(first, 2)
        turned = turn(first)
        staged = z[:, last, HALF : HALF + P]
        nc.scalar.copy(out=staged, in_=turned[:])
        back = psum.tile([P, G], F32, name="back", tag="bank%d" % (2 * first))
        nc.tensor.transpose(back[:], staged, ident[:])
        nc.scalar.copy(out=b_bf[:, :, first], in_=back[:])
        nc.scalar.copy(out=z[:, last, HALF:], in_=held[:])

        products(second, 1)
        turned = turn(second)
        staged_second = keep.tile([G, P], F32, name="staged_second")
        nc.scalar.copy(out=staged_second[:], in_=turned[:])
        products(third, 1)
        turned = turn(third)

        wo_bf = [keep.tile([P, FH * PACK], BF16, name="wo_bf%d" % h, align_bytes=64) for h in range(2)]
        products(last, 2)
        interleave(wo_raw[0], wo_bf[0], 0)
        staged = wo_raw[0][:, 0, :P]
        nc.scalar.copy(out=staged, in_=turned[:])
        src = wo_raw[1][:].rearrange("p j (c i) -> p c j i", i=4)
        dst = wo_bf[1][:].rearrange("p (c i j) -> p c j i", i=4, j=PACK)
        nc.scalar.copy(out=dst[:, : P // 4], in_=src[:, : P // 4])
        nc.gpsimd.tensor_scalar(
            wo_bf[1][:].rearrange("p (f j) -> p f j", j=PACK)[:, P:],
            wo_raw[1][:].rearrange("p j f -> p f j")[:, P:],
            1.0,
            0.0,
            MULT,
            ADD,
        )
        back = psum.tile([P, 2, G], F32, name="back", tag="bank%d" % (2 * third))
        nc.tensor.transpose(back[:, 0, :], staged_second[:], ident[:])
        nc.tensor.transpose(back[:, 1, :], staged, ident[:])
        nc.scalar.copy(out=b_bf[:, :, 0:2], in_=back[:].rearrange("p t g -> p g t"))
        with nc.allow_low_precision(reason="float32 sum, rounded once for the quantiser"):
            for h in range(2):
                nc.vector.tensor_reduce(
                    out=b_bf[:, h * G // 2 : (h + 1) * G // 2, last],
                    in_=x[last][:, h * HALF : (h + 1) * HALF].rearrange("p (g e) -> p g e", e=EDGES),
                    axis=AXIS_X,
                    op=ADD,
                )
        wo_q0 = quantize(wo_bf[0][:], FH, "wo0")
        wo_q1 = quantize(wo_bf[1][:], FH, "wo1")
        b_codes, b_scales = quantize(b_bf[:].rearrange("p g t -> p (g t)"), G, "b")

        out_rows = out.rearrange("(j p) g -> p j g", p=P)
        def output_tile(acc, wo_q, j):
            codes, scales = wo_q
            nc.tensor.matmul_mx(
                out=acc,
                lhsT=codes[:, j * P : (j + 1) * P].bitcast(FP8X4),
                lhsT_scale=scales[:, j * P : (j + 1) * P],
                rhs=b_codes[:].bitcast(FP8X4),
                rhs_scale=b_scales[:],
                start=True,
                stop=True,
            )

        y = [keep.tile([P, 2, G], F32, name="y%d" % h) for h in range(2)]
        bank = psum.tile([P, 2, G], F32, name="ybank", tag="bank1")
        for j in range(2):
            output_tile(bank[:, j, :], wo_q0, j)
        nc.scalar.copy(out=y[0][:], in_=bank[:])
        nc.sync.dma_start(out=out_rows[:, 0:2, :], in_=y[0][:])
        for j in range(2):
            bank = psum.tile([P, G], F32, name="ybank", tag="bank%d" % (3 + 2 * j))
            output_tile(bank[:], wo_q1, j)
            if j == 0:
                nc.vector.tensor_copy(out=y[1][:, j, :], in_=bank[:])
            else:
                nc.scalar.copy(out=y[1][:, j, :], in_=bank[:])
        nc.sync.dma_start(out=out_rows[:, 2:4, :], in_=y[1][:])
